import numpy as np
import ml_dtypes


def mxq(x, axis, fmt="e4m3"):
    dtype, down = {"e4m3": (ml_dtypes.float8_e4m3fn, 7), "e5m2": (ml_dtypes.float8_e5m2, 14)}[fmt]
    v = np.moveaxis(np.asarray(x, np.float32).astype(ml_dtypes.bfloat16).astype(np.float64), axis, -1)
    blocks = v.reshape(v.shape[:-1] + (-1, 32))
    amax = np.abs(blocks).max(-1, keepdims=True)
    byte = np.maximum(np.where(amax > 0, np.frexp(amax)[1] - 1 + 127, 0) - down, 1)
    scale = np.exp2(byte - 127.0)
    codes = (blocks / scale).astype(np.float32).astype(dtype).astype(np.float64)
    return np.moveaxis((codes * scale).reshape(v.shape), -1, axis)


WIDE = False


def mx_kscale(k):
    if not WIDE:
        return np.ones(k)
    levels = np.array([10, -10, 5, -5, 0])
    if k % 512:
        return np.exp2(np.random.permutation(np.resize(levels, k // 32))).repeat(32)
    a = np.empty((k // 512, 16))
    for p in range(k // 512):
        a[p, :8] = np.random.permutation(np.resize(levels, 8))
        for g in range(8):
            far = levels[np.abs(levels - a[p, g]) >= 10]
            a[p, g + 8] = far[np.random.randint(len(far))]
    return np.exp2(a.ravel()).repeat(32)


def f64(x):
    return np.asarray(x).astype(np.float64)


def striped(idx):
    return np.tile(idx.reshape(-1, 16).T, (8, 1)).astype(np.uint16)


def unstriped(offs):
    return offs[:16].T.reshape(-1).astype(np.int64)


E2M1 = np.array([0.0, 0.5, 1.0, 1.5, 2.0, 3.0, 4.0, 6.0, -0.0, -0.5, -1.0, -1.5, -2.0, -3.0, -4.0, -6.0])


def pack_weight(w, fmt):
    k, n = w.shape
    w = f64(np.asarray(w, np.float32).astype(ml_dtypes.bfloat16)).reshape(k // 32, 32, n)
    amax = np.abs(w).max(1)
    if fmt == "e4m3":
        byte = np.frexp(amax)[1] - 1 + 127 - 7
    else:
        mant, ex = np.frexp(amax / 6.0)
        byte = np.where(mant > 0.5, ex, ex - 1) + 127
    byte = np.clip(np.where(amax > 0, byte, 1), 1, 254)
    scaled = (w * np.exp2(127.0 - byte)[:, None, :]).reshape(k, n).astype(np.float32)
    by_word = np.ascontiguousarray(scaled.reshape(k // 512, 128, 4, n).transpose(0, 1, 3, 2))
    if fmt == "e4m3":
        words = by_word.astype(ml_dtypes.float8_e4m3fn).view(np.uint8)
    else:
        c = by_word.astype(ml_dtypes.float4_e2m1fn).view(np.uint8) & 0xF
        words = (c[..., 0::2] | (c[..., 1::2] << 4)).reshape(k // 512, 128, 2 * n)
    return np.ascontiguousarray(words), np.ascontiguousarray(byte.astype(np.uint8).reshape(k // 512, 16, n))


def unpack_weight(words, scales, fmt):
    g, _, n = scales.shape
    words = np.ascontiguousarray(words).reshape(g, 128, n, -1)
    if fmt == "e4m3":
        vals = words.view(ml_dtypes.float8_e4m3fn).astype(np.float64)
    else:
        nib = np.empty((g, 128, n, 4), np.uint8)
        nib[..., 0::2] = words & 0xF
        nib[..., 1::2] = words >> 4
        vals = E2M1[nib]
    vals = vals * np.repeat(np.exp2(scales.astype(np.float64) - 127.0), 8, axis=1)[..., None]
    return vals.transpose(0, 1, 3, 2).reshape(g * 512, n)


def gelu(v):
    return 0.5 * v * (1.0 + np.tanh(np.sqrt(2.0 / np.pi) * (v + 0.044715 * v**3)))


K, T, S, H, T3, S2, P = 1536, 2048, 1024, 1024, 2048, 512, 512

def setup_inputs():
    n = np.random.standard_normal
    sc = mx_kscale(K)[:, None]
    u = mx_kscale(H)[:, None]
    tab_words, tab_scales = pack_weight(n((K, T)) * sc, "e4m3")
    tab2_words, tab2_scales = pack_weight(n((H, T3)) / np.sqrt(H) / u, "e4m3")
    w4_words, w4_scales = pack_weight(n((H, S2)) / np.sqrt(H) / u, "e2m1")
    return {
        "tab_words": tab_words, "tab_scales": tab_scales,
        "offs": striped(np.random.permutation(T)[:S]),
        "w1": (1.2 * n((K, H)) / np.sqrt(K) / sc).astype(np.float32),
        "b1": (0.5 * n(H)).astype(np.float32),
        "gain": (np.random.uniform(0.8, 1.6, H) * u[:, 0]).astype(np.float32),
        "tab2_words": tab2_words, "tab2_scales": tab2_scales,
        "offs2": striped(np.random.permutation(T3)[:S2]),
        "w4_words": w4_words, "w4_scales": w4_scales,
        "pos1": striped(np.random.permutation(S)[:P]),
        "pos2": striped(np.random.permutation(S)[:P]),
        "temp": np.random.uniform(0.4, 1.6, S2).astype(np.float32),
        "kin": (0.2 * n(S2)).astype(np.float32),
    }

def reference(tab_words, tab_scales, offs, w1, b1, gain, tab2_words, tab2_scales, offs2, w4_words, w4_scales, pos1, pos2, temp, kin):
    v = unpack_weight(tab_words, tab_scales, "e4m3")[:, unstriped(offs)]
    v2 = unpack_weight(tab2_words, tab2_scales, "e4m3")[:, unstriped(offs2)]
    w4 = unpack_weight(w4_words, w4_scales, "e2m1")
    f = mxq(f64(w1), 0, "e4m3").T @ v
    h = f64(gain)[:, None] * np.tanh(f + f64(b1)[:, None])
    hq = mxq(h, 0, "e4m3")
    d = w4.T @ hq
    e = np.maximum(v2.T @ hq, d)
    top = e.max(axis=1)
    a = np.exp(f64(temp)[:, None] * (e[:, unstriped(pos1)] - top[:, None]))
    return a * d[:, unstriped(pos2)] + f64(kin)[:, None]

@@ -1,0 +1,303 @@
+from contextlib import ExitStack
+
+import concourse.mybir as mybir
+
+K, T, S, H, T3, S2, NP = 1536, 2048, 1024, 1024, 2048, 512, 512
+FLOPS = 2 * K * H * S + 2 * 2 * H * S2 * S
+
+F32 = mybir.dt.float32
+BF16 = mybir.dt.bfloat16
+I32 = mybir.dt.int32
+U32 = mybir.dt.uint32
+U16 = mybir.dt.uint16
+U8 = mybir.dt.uint8
+FP8X4 = mybir.dt.float8_e4m3fn_x4
+FP4X4 = mybir.dt.float4_e2m1fn_x4
+ALU = mybir.AluOpType
+ACT = mybir.ActivationFunctionType
+
+P = 128
+PACK = 4
+KP = 512
+N = 512
+KA = K // KP
+HB = H // KP
+JH = S // N
+MT = S2 // P
+
+
+def tile_list_gravestone_kin_scores_kernel(
+    tc, tab_words, tab_scales, offs, w1, b1, gain, tab2_words, tab2_scales, offs2,
+    w4_words, w4_scales, pos1, pos2, temp, kin, out,
+):
+    nc = tc.nc
+    with ExitStack() as ctx:
+        keep = ctx.enter_context(tc.tile_pool(name="keep", bufs=1))
+        ring = ctx.enter_context(tc.tile_pool(name="ring", bufs=2))
+        psum = ctx.enter_context(tc.psum_pool(name="psum", bufs=1))
+
+        def held(name, shape, dtype):
+            return keep.tile(shape, dtype, name=name, align_bytes=64)
+
+        def bank(k):
+            return psum.tile([P, N], F32, name=f"bank{k}", tag=f"bank{k}")
+
+        offs_t = held("offs_t", [P, S // 16], U16)
+        offs2_t = held("offs2_t", [P, S2 // 16], U16)
+        pos1_t = held("pos1_t", [P, NP // 16], U16)
+        pos2_t = held("pos2_t", [P, NP // 16], U16)
+
+        tab_w = [held(f"tab_w{a}", [P, T], U32) for a in range(KA)]
+        tab_s = held("tab_s", [P, T], U8)
+        tab2_w = [held(f"tab2_w{b}", [P, T3], U32) for b in range(HB)]
+        tab2_s = held("tab2_s", [P, T3], U8)
+        w4_w = [held(f"w4_w{b}", [P, 2 * S2], U8) for b in range(HB)]
+        w4_s = held("w4_s", [P, HB * S2], U8)
+        b1_t = held("b1_t", [P, HB * PACK], F32)
+        gain_t = held("gain_t", [P, HB * PACK], F32)
+        temp_t = held("temp_t", [P, MT], F32)
+        kin_t = held("kin_t", [P, MT], F32)
+        bias_t = held("bias_t", [P, MT], F32)
+
+        v_w = {(a, j): held(f"v_w{a}{j}", [P, N], U32) for a in range(KA) for j in range(JH)}
+        v_s = [held(f"v_s{j}", [P, N], U8) for j in range(JH)]
+        v2_w = [held(f"v2_w{b}", [P, S2], U32) for b in range(HB)]
+        v2_s = held("v2_s", [P, S2], U8)
+        w_c = {(b, a): held(f"w_c{b}{a}", [P, KP], U32) for b in range(HB) for a in range(KA)}
+        w_s = {(b, a): held(f"w_s{b}{a}", [P, KP], U8) for b in range(HB) for a in range(KA)}
+        h_c = {(b, j): held(f"h_c{b}{j}", [P, N], U32) for b in range(HB) for j in range(JH)}
+        h_s = {(b, j): held(f"h_s{b}{j}", [P, N], U8) for b in range(HB) for j in range(JH)}
+        d_t = [held(f"d_t{m}", [P, S], F32) for m in range(MT)]
+        e_t = [held(f"e_t{m}", [P, S], F32) for m in range(MT)]
+
+        w_raw, w_bf, th, hp, hb, acc1, acc2, look = {}, {}, {}, {}, {}, {}, {}, {}
+
+        def words(dram):
+            return dram.rearrange("p t i -> p (t i)").bitcast(I32)
+
+        def load_w(b, a, pieces=1):
+            width = KP // pieces
+            for x in range(pieces):
+                w_raw[b, a, x] = ring.tile([P, PACK, width], F32, name=f"w_raw{pieces}", bufs=4)
+                c0 = b * KP + x * width
+                nc.sync.dma_start(
+                    out=w_raw[b, a, x][:],
+                    in_=w1[a * KP : (a + 1) * KP, c0 : c0 + width].rearrange("(p i) c -> p i c", i=PACK),
+                )
+
+        def cast_w(b, a, engines):
+            w_bf[b, a] = ring.tile([P, PACK * KP], BF16, name="w_bf", bufs=3, align_bytes=64)
+            rows = P // len(engines)
+            for x, engine in enumerate(engines):
+                src = w_raw[b, a, x][:].rearrange("p i (m t) -> p m i t", t=PACK)
+                dst = w_bf[b, a][:].rearrange("p (t m i) -> p m i t", t=PACK, i=PACK)[:, x * rows : (x + 1) * rows]
+                if engine == "scalar":
+                    nc.scalar.copy(out=dst, in_=src)
+                else:
+                    nc.vector.tensor_copy(out=dst, in_=src)
+
+        def quant_w(b, a):
+            nc.vector.quantize_mx(out=w_c[b, a][:].bitcast(FP8X4), scales=w_s[b, a][:], in_=w_bf[b, a][:])
+
+        def half(j):
+            return slice(j * N // 16, (j + 1) * N // 16)
+
+        def gather_words(a, j):
+            nc.vector.tensor_copy(out=v_w[a, j][:], in_=tab_w[a][:].indirect(offs_t[:, half(j)]))
+
+        def gather_scales(j):
+            nc.vector.tensor_copy(out=v_s[j][:], in_=tab_s[:].indirect(offs_t[:, half(j)]))
+
+        def mm1(b, j, t, a):
+            if a == 0:
+                acc1[b, j, t] = bank(PACK * j + t)
+            cols = slice(t * P, (t + 1) * P)
+            nc.tensor.matmul_mx(
+                out=acc1[b, j, t][:],
+                lhsT=w_c[b, a][:, cols].bitcast(FP8X4),
+                lhsT_scale=w_s[b, a][:, cols],
+                rhs=v_w[a, j][:].bitcast(FP8X4),
+                rhs_scale=v_s[j][4 * a : P, :],
+                start=(a == 0),
+                stop=(a == KA - 1),
+            )
+
+        def tanh(b, j):
+            th[b, j] = ring.tile([P, PACK, N], F32, name="th", bufs=2)
+            for t in range(PACK):
+                c = b * PACK + t
+                nc.scalar.activation(out=th[b, j][:, t, :], in_=acc1[b, j, t][:], func=ACT.Tanh, bias=b1_t[:, c : c + 1])
+
+        def apply_gain(b, j):
+            hb[b, j] = ring.tile([P, PACK * N], BF16, name="hb", bufs=2, align_bytes=64)
+            g = gain_t[:, b * PACK : (b + 1) * PACK].rearrange("p (c t u) -> p c t u", c=1, u=1)
+            nc.vector.tensor_tensor(
+                out=hb[b, j][:].rearrange("p (c u t) -> p c t u", t=PACK, u=4),
+                in0=th[b, j][:].rearrange("p t (c u) -> p c t u", u=4),
+                in1=g.to_broadcast([P, N // 4, PACK, 4]),
+                op=ALU.mult,
+            )
+
+        def gain_on_scalar(b, j):
+            hp[b, j] = ring.tile([P, PACK, N], BF16, name="hp", bufs=2)
+            for t in range(PACK):
+                c = b * PACK + t
+                nc.scalar.activation(out=hp[b, j][:, t, :], in_=th[b, j][:, t, :], func=ACT.Copy, scale=gain_t[:, c : c + 1])
+
+        def interleave(b, j):
+            hb[b, j] = ring.tile([P, PACK * N], BF16, name="hb", bufs=2, align_bytes=64)
+            nc.vector.tensor_copy(
+                out=hb[b, j][:].rearrange("p (c u t) -> p c t u", t=PACK, u=4),
+                in_=hp[b, j][:].rearrange("p t (c u) -> p c t u", u=4),
+            )
+
+        def quant_h(b, j):
+            nc.vector.quantize_mx(out=h_c[b, j][:].bitcast(FP8X4), scales=h_s[b, j][:], in_=hb[b, j][:])
+
+        def mm2(m, j, kind, b):
+            if b == 0:
+                acc2[m, j, kind] = bank(2 * m + kind)
+            cols = slice(m * P, (m + 1) * P)
+            if kind == 0:
+                lhsT = w4_w[b][:, 2 * m * P : 2 * (m + 1) * P].bitcast(FP4X4)
+                lhsT_scale = w4_s[:, b * S2 + m * P : b * S2 + (m + 1) * P]
+            else:
+                lhsT = v2_w[b][:, cols].bitcast(FP8X4)
+                lhsT_scale = v2_s[4 * b : P, cols]
+            nc.tensor.matmul_mx(
+                out=acc2[m, j, kind][:],
+                lhsT=lhsT,
+                lhsT_scale=lhsT_scale,
+                rhs=h_c[b, j][:].bitcast(FP8X4),
+                rhs_scale=h_s[b, j][:],
+                start=(b == 0),
+                stop=(b == HB - 1),
+            )
+
+        def take_d(m, j):
+            nc.scalar.copy(out=d_t[m][:, j * N : (j + 1) * N], in_=acc2[m, j, 0][:])
+
+        def take_e(m, j):
+            cols = slice(j * N, (j + 1) * N)
+            nc.vector.tensor_tensor(out=e_t[m][:, cols], in0=acc2[m, j, 1][:], in1=d_t[m][:, cols], op=ALU.max)
+
+        def row_max(m):
+            top = ring.tile([P, 1], F32, name="top")
+            nc.vector.reduce_max(out=top[:], in_=e_t[m][:], axis=mybir.AxisListType.X)
+            nc.vector.tensor_scalar(
+                out=bias_t[:, m : m + 1], in0=top[:], scalar1=temp_t[:, m : m + 1], scalar2=-1.0,
+                op0=ALU.mult, op1=ALU.mult,
+            )
+
+        def exp_look(m):
+            look[m] = ring.tile([P, NP], F32, name="look")
+            nc.scalar.activation(
+                out=look[m][:], in_=e_t[m][:].indirect(pos1_t[:]), func=ACT.Exp,
+                bias=bias_t[:, m : m + 1], scale=temp_t[:, m : m + 1],
+            )
+
+        def finish(m):
+            prod = ring.tile([P, NP], F32, name="prod")
+            nc.vector.tensor_tensor(out=prod[:], in0=d_t[m][:].indirect(pos2_t[:]), in1=look[m][:], op=ALU.mult)
+            res = ring.tile([P, NP], F32, name="res")
+            nc.scalar.activation(out=res[:], in_=prod[:], func=ACT.Identity, bias=kin_t[:, m : m + 1])
+            nc.sync.dma_start(out=out[m * P : (m + 1) * P, :], in_=res[:])
+
+        nc.gpsimd.memset(tab_s[:].bitcast(I32), 0)
+        nc.vector.memset(tab2_s[:].bitcast(I32), 0)
+        nc.vector.memset(w4_s[:].bitcast(I32), 0)
+        nc.sync.dma_start(offs_t[:], offs)
+        nc.sync.dma_start(out=tab_w[0][:].bitcast(I32), in_=words(tab_words[0]))
+        for q in range(4):
+            nc.sync.dma_start(
+                out=tab_s[32 * q : 32 * q + 4 * KA, :].bitcast(I32),
+                in_=tab_scales[:, 4 * q : 4 * q + 4, :].bitcast(I32),
+            )
+        load_w(0, 0)
+        nc.sync.dma_start(out=tab_w[1][:].bitcast(I32), in_=words(tab_words[1]))
+        load_w(0, 1)
+        nc.sync.dma_start(out=tab_w[2][:].bitcast(I32), in_=words(tab_words[2]))
+        load_w(0, 2, 2)
+        load_w(1, 0)
+        nc.sync.dma_start(out=b1_t[:].rearrange("p (b i) -> p b i", i=PACK), in_=b1.rearrange("(b p i) -> p b i", p=P, i=PACK))
+        nc.sync.dma_start(out=gain_t[:].rearrange("p (b i) -> p b i", i=PACK), in_=gain.rearrange("(b p i) -> p b i", p=P, i=PACK))
+
+        for a in range(KA):
+            gather_words(a, 0)
+            gather_words(a, 1)
+            if a == 0:
+                gather_scales(0)
+                gather_scales(1)
+            cast_w(0, a, ["scalar"] if a < KA - 1 else ["scalar", "vector"])
+            quant_w(0, a)
+            for j in range(JH):
+                for t in range(PACK):
+                    mm1(0, j, t, a)
+        load_w(1, 1)
+        load_w(1, 2, 2)
+        nc.sync.dma_start(offs2_t[:], offs2)
+        nc.sync.dma_start(out=tab2_w[0][:].bitcast(I32), in_=words(tab2_words[0]))
+        for q in range(4):
+            nc.sync.dma_start(
+                out=tab2_s[32 * q : 32 * q + 4 * HB, :].bitcast(I32),
+                in_=tab2_scales[:, 4 * q : 4 * q + 4, :].bitcast(I32),
+            )
+        nc.sync.dma_start(out=tab2_w[1][:].bitcast(I32), in_=words(tab2_words[1]))
+        for b in range(HB):
+            nc.sync.dma_start(out=w4_w[b][:].bitcast(I32), in_=w4_words[b].bitcast(I32))
+        for q in range(4):
+            nc.sync.dma_start(
+                out=w4_s[32 * q : 32 * q + 4, :].bitcast(I32).rearrange("r (b c) -> r b c", b=HB),
+                in_=w4_scales[:, 4 * q : 4 * q + 4, :].bitcast(I32).rearrange("b r c -> r b c"),
+            )
+        nc.sync.dma_start(pos1_t[:], pos1)
+        nc.sync.dma_start(pos2_t[:], pos2)
+        with nc.allow_non_contiguous_dma(reason="one value a partition"):
+            nc.sync.dma_start(out=temp_t[:], in_=temp.rearrange("(m p) -> p m", p=P))
+            nc.sync.dma_start(out=kin_t[:], in_=kin.rearrange("(m p) -> p m", p=P))
+
+        tanh(0, 0)
+        cast_w(1, 0, ["vector"])
+        quant_w(1, 0)
+        tanh(0, 1)
+        apply_gain(0, 0)
+        cast_w(1, 1, ["scalar"])
+        cast_w(1, 2, ["vector", "vector"])
+        quant_h(0, 0)
+        quant_w(1, 2)
+        quant_w(1, 1)
+        for j in range(JH):
+            for t in range(PACK):
+                for a in range(KA):
+                    mm1(1, j, t, a)
+        gain_on_scalar(0, 1)
+        tanh(1, 0)
+        nc.vector.tensor_copy(out=v2_w[0][:], in_=tab2_w[0][:].indirect(offs2_t[:]))
+        interleave(0, 1)
+        gain_on_scalar(1, 0)
+        nc.vector.tensor_copy(out=v2_s[:], in_=tab2_s[:].indirect(offs2_t[:]))
+        quant_h(0, 1)
+        tanh(1, 1)
+        nc.vector.tensor_copy(out=v2_w[1][:], in_=tab2_w[1][:].indirect(offs2_t[:]))
+        interleave(1, 0)
+        quant_h(1, 0)
+        apply_gain(1, 1)
+        for m in range(MT):
+            for kind in range(2):
+                for b in range(HB):
+                    mm2(m, 0, kind, b)
+            take_d(m, 0)
+        quant_h(1, 1)
+        for m in range(MT):
+            take_e(m, 0)
+        for m in range(MT):
+            for kind in range(2):
+                for b in range(HB):
+                    mm2(m, 1, kind, b)
+            take_d(m, 1)
+            take_e(m, 1)
+            row_max(m)
+            exp_look(m)
+            if m > 0:
+                finish(m - 1)
+        finish(MT - 1)

@@ -58,9 +58,11 @@ def tile_list_gravestone_kin_scores_kernel(
         temp_t = held("temp_t", [P, MT], F32)
         kin_t = held("kin_t", [P, MT], F32)
         bias_t = held("bias_t", [P, MT], F32)
+        ntemp_t = held("ntemp_t", [P, MT], F32)
+        top_t = [held(f"top_t{m}", [P, 1], F32) for m in range(MT)]
 
-        v_w = {(a, j): held(f"v_w{a}{j}", [P, N], U32) for a in range(KA) for j in range(JH)}
-        v_s = [held(f"v_s{j}", [P, N], U8) for j in range(JH)]
+        v_w = [held(f"v_w{a}", [P, S], U32) for a in range(KA)]
+        v_s = held("v_s", [P, S], U8)
         v2_w = [held(f"v2_w{b}", [P, S2], U32) for b in range(HB)]
         v2_s = held("v2_s", [P, S2], U8)
         w_c = {(b, a): held(f"w_c{b}{a}", [P, KP], U32) for b in range(HB) for a in range(KA)}
@@ -78,7 +80,8 @@ def tile_list_gravestone_kin_scores_kernel(
         def load_w(b, a, pieces=1):
             width = KP // pieces
             for x in range(pieces):
-                w_raw[b, a, x] = ring.tile([P, PACK, width], F32, name=f"w_raw{pieces}", bufs=4)
+                tag, bufs = ("w_last0", 1) if (b, a, x) == (1, KA - 1, 1) else (f"w_raw{pieces}", 4)
+                w_raw[b, a, x] = ring.tile([P, PACK, width], F32, name="w_raw", tag=tag, bufs=bufs)
                 c0 = b * KP + x * width
                 nc.sync.dma_start(
                     out=w_raw[b, a, x][:],
@@ -86,10 +89,14 @@ def tile_list_gravestone_kin_scores_kernel(
                 )
 
         def cast_w(b, a, engines):
-            w_bf[b, a] = ring.tile([P, PACK * KP], BF16, name="w_bf", bufs=3, align_bytes=64)
+            tag, bufs = ("w_bf10", 1) if (b, a) == (1, 0) else ("w_bf", 3)
+            w_bf[b, a] = ring.tile([P, PACK * KP], BF16, name="w_bf", tag=tag, bufs=bufs, align_bytes=64)
             rows = P // len(engines)
             for x, engine in enumerate(engines):
-                src = w_raw[b, a, x][:].rearrange("p i (m t) -> p m i t", t=PACK)
+                if (b, a, 1) in w_raw:
+                    src = w_raw[b, a, x][:].rearrange("p i (m t) -> p m i t", t=PACK)
+                else:
+                    src = w_raw[b, a, 0][:].rearrange("p i (m t) -> p m i t", t=PACK)[:, x * rows : (x + 1) * rows]
                 dst = w_bf[b, a][:].rearrange("p (t m i) -> p m i t", t=PACK, i=PACK)[:, x * rows : (x + 1) * rows]
                 if engine == "scalar":
                     nc.scalar.copy(out=dst, in_=src)
@@ -99,14 +106,17 @@ def tile_list_gravestone_kin_scores_kernel(
         def quant_w(b, a):
             nc.vector.quantize_mx(out=w_c[b, a][:].bitcast(FP8X4), scales=w_s[b, a][:], in_=w_bf[b, a][:])
 
-        def half(j):
-            return slice(j * N // 16, (j + 1) * N // 16)
+        def quant_w_slot(b, a, t):
+            nc.vector.quantize_mx(
+                out=w_c[b, a][:, t * P : (t + 1) * P].bitcast(FP8X4),
+                scales=w_s[b, a][:, t * P : (t + 1) * P],
+                in_=w_bf[b, a][:, t * KP : (t + 1) * KP],
+            )
 
-        def gather_words(a, j):
-            nc.vector.tensor_copy(out=v_w[a, j][:], in_=tab_w[a][:].indirect(offs_t[:, half(j)]))
-
-        def gather_scales(j):
-            nc.vector.tensor_copy(out=v_s[j][:], in_=tab_s[:].indirect(offs_t[:, half(j)]))
+        def gather_words(a, j0, j1):
+            nc.vector.tensor_copy(
+                out=v_w[a][:, j0 * N : j1 * N], in_=tab_w[a][:].indirect(offs_t[:, j0 * N // 16 : j1 * N // 16])
+            )
 
         def mm1(b, j, t, a):
             if a == 0:
@@ -116,20 +126,21 @@ def tile_list_gravestone_kin_scores_kernel(
                 out=acc1[b, j, t][:],
                 lhsT=w_c[b, a][:, cols].bitcast(FP8X4),
                 lhsT_scale=w_s[b, a][:, cols],
-                rhs=v_w[a, j][:].bitcast(FP8X4),
-                rhs_scale=v_s[j][4 * a : P, :],
+                rhs=v_w[a][:, j * N : (j + 1) * N].bitcast(FP8X4),
+                rhs_scale=v_s[4 * a : P, j * N : (j + 1) * N],
                 start=(a == 0),
                 stop=(a == KA - 1),
             )
 
         def tanh(b, j):
-            th[b, j] = ring.tile([P, PACK, N], F32, name="th", bufs=2)
+            th[b, j] = ring.tile([P, PACK, N], F32, name="th", bufs=3)
             for t in range(PACK):
                 c = b * PACK + t
                 nc.scalar.activation(out=th[b, j][:, t, :], in_=acc1[b, j, t][:], func=ACT.Tanh, bias=b1_t[:, c : c + 1])
 
         def apply_gain(b, j):
-            hb[b, j] = ring.tile([P, PACK * N], BF16, name="hb", bufs=2, align_bytes=64)
+            tag, bufs = ("w_bf10", 1) if (b, j) == (0, 0) else ("hb", 2)
+            hb[b, j] = ring.tile([P, PACK * N], BF16, name="hb", tag=tag, bufs=bufs, align_bytes=64)
             g = gain_t[:, b * PACK : (b + 1) * PACK].rearrange("p (c t u) -> p c t u", c=1, u=1)
             nc.vector.tensor_tensor(
                 out=hb[b, j][:].rearrange("p (c u t) -> p c t u", t=PACK, u=4),
@@ -138,14 +149,19 @@ def tile_list_gravestone_kin_scores_kernel(
                 op=ALU.mult,
             )
 
-        def gain_on_scalar(b, j):
-            hp[b, j] = ring.tile([P, PACK, N], BF16, name="hp", bufs=2)
+        def gain_on_scalar(b, j, on_vector):
+            hp[b, j] = ring.tile([P, PACK, N], BF16, name="hp", tag=f"w_last{b}", bufs=1)
             for t in range(PACK):
                 c = b * PACK + t
-                nc.scalar.activation(out=hp[b, j][:, t, :], in_=th[b, j][:, t, :], func=ACT.Copy, scale=gain_t[:, c : c + 1])
+                if t < PACK - on_vector:
+                    nc.scalar.activation(out=hp[b, j][:, t, :], in_=th[b, j][:, t, :], func=ACT.Copy, scale=gain_t[:, c : c + 1])
+                else:
+                    nc.vector.tensor_scalar(
+                        out=hp[b, j][:, t, :], in0=th[b, j][:, t, :], scalar1=gain_t[:, c : c + 1], scalar2=None, op0=ALU.mult
+                    )
 
         def interleave(b, j):
-            hb[b, j] = ring.tile([P, PACK * N], BF16, name="hb", bufs=2, align_bytes=64)
+            hb[b, j] = ring.tile([P, PACK * N], BF16, name="hb", tag="hb", bufs=2, align_bytes=64)
             nc.vector.tensor_copy(
                 out=hb[b, j][:].rearrange("p (c u t) -> p c t u", t=PACK, u=4),
                 in_=hp[b, j][:].rearrange("p t (c u) -> p c t u", u=4),
@@ -182,55 +198,64 @@ def tile_list_gravestone_kin_scores_kernel(
             nc.vector.tensor_tensor(out=e_t[m][:, cols], in0=acc2[m, j, 1][:], in1=d_t[m][:, cols], op=ALU.max)
 
         def row_max(m):
-            top = ring.tile([P, 1], F32, name="top")
-            nc.vector.reduce_max(out=top[:], in_=e_t[m][:], axis=mybir.AxisListType.X)
-            nc.vector.tensor_scalar(
-                out=bias_t[:, m : m + 1], in0=top[:], scalar1=temp_t[:, m : m + 1], scalar2=-1.0,
-                op0=ALU.mult, op1=ALU.mult,
-            )
+            nc.vector.reduce_max(out=top_t[m][:], in_=e_t[m][:], axis=mybir.AxisListType.X)
+
+        def make_bias(m):
+            nc.scalar.activation(out=bias_t[:, m : m + 1], in_=top_t[m][:], func=ACT.Copy, scale=ntemp_t[:, m : m + 1])
 
         def exp_look(m):
-            look[m] = ring.tile([P, NP], F32, name="look")
+            look[m] = ring.tile([P, NP], F32, name="look", tag="w_raw2", bufs=4)
             nc.scalar.activation(
                 out=look[m][:], in_=e_t[m][:].indirect(pos1_t[:]), func=ACT.Exp,
                 bias=bias_t[:, m : m + 1], scale=temp_t[:, m : m + 1],
             )
 
-        def finish(m):
-            prod = ring.tile([P, NP], F32, name="prod")
-            nc.vector.tensor_tensor(out=prod[:], in0=d_t[m][:].indirect(pos2_t[:]), in1=look[m][:], op=ALU.mult)
-            res = ring.tile([P, NP], F32, name="res")
-            nc.scalar.activation(out=res[:], in_=prod[:], func=ACT.Identity, bias=kin_t[:, m : m + 1])
-            nc.sync.dma_start(out=out[m * P : (m + 1) * P, :], in_=res[:])
+        def finish(m, cuts=(0, NP)):
+            for c0, c1 in zip(cuts, cuts[1:]):
+                width = c1 - c0
+                cols = slice(c0, c1)
+                prod = ring.tile([P, width], F32, name="prod", tag="w_raw1", bufs=4)
+                nc.vector.tensor_tensor(
+                    out=prod[:], in0=d_t[m][:].indirect(pos2_t[:, c0 // 16 : c1 // 16]),
+                    in1=look[m][:, cols], op=ALU.mult,
+                )
+                res = ring.tile([P, width], F32, name="res", bufs=5)
+                nc.scalar.activation(out=res[:], in_=prod[:], func=ACT.Identity, bias=kin_t[:, m : m + 1])
+                nc.sync.dma_start(out=out[m * P : (m + 1) * P, cols], in_=res[:])
 
         nc.gpsimd.memset(tab_s[:].bitcast(I32), 0)
-        nc.vector.memset(tab2_s[:].bitcast(I32), 0)
-        nc.vector.memset(w4_s[:].bitcast(I32), 0)
-        nc.sync.dma_start(offs_t[:], offs)
+        nc.gpsimd.memset(tab2_s[:].bitcast(I32), 0)
+        nc.gpsimd.memset(w4_s[:].bitcast(I32), 0)
         nc.sync.dma_start(out=tab_w[0][:].bitcast(I32), in_=words(tab_words[0]))
+        nc.sync.dma_start(offs_t[:], offs)
+        load_w(0, 0)
         for q in range(4):
             nc.sync.dma_start(
                 out=tab_s[32 * q : 32 * q + 4 * KA, :].bitcast(I32),
                 in_=tab_scales[:, 4 * q : 4 * q + 4, :].bitcast(I32),
             )
-        load_w(0, 0)
         nc.sync.dma_start(out=tab_w[1][:].bitcast(I32), in_=words(tab_words[1]))
         load_w(0, 1)
         nc.sync.dma_start(out=tab_w[2][:].bitcast(I32), in_=words(tab_words[2]))
         load_w(0, 2, 2)
-        load_w(1, 0)
         nc.sync.dma_start(out=b1_t[:].rearrange("p (b i) -> p b i", i=PACK), in_=b1.rearrange("(b p i) -> p b i", p=P, i=PACK))
+        load_w(1, 0)
         nc.sync.dma_start(out=gain_t[:].rearrange("p (b i) -> p b i", i=PACK), in_=gain.rearrange("(b p i) -> p b i", p=P, i=PACK))
 
-        for a in range(KA):
-            gather_words(a, 0)
-            gather_words(a, 1)
-            if a == 0:
-                gather_scales(0)
-                gather_scales(1)
-            cast_w(0, a, ["scalar"] if a < KA - 1 else ["scalar", "vector"])
-            quant_w(0, a)
-            for j in range(JH):
+        gather_words(0, 0, JH)
+        nc.vector.tensor_copy(out=v_s[:], in_=tab_s[:].indirect(offs_t[:]))
+        cast_w(0, 0, ["scalar"])
+        quant_w(0, 0)
+        gather_words(1, 0, JH)
+        cast_w(0, 1, ["scalar", "vector"])
+        quant_w(0, 1)
+        gather_words(2, 0, 1)
+        cast_w(0, 2, ["scalar", "scalar"])
+        for t in range(PACK):
+            quant_w_slot(0, KA - 1, t)
+        gather_words(2, 1, 2)
+        for j in range(JH):
+            for a in range(KA):
                 for t in range(PACK):
                     mm1(0, j, t, a)
         load_w(1, 1)
@@ -261,33 +286,35 @@ def tile_list_gravestone_kin_scores_kernel(
         quant_w(1, 0)
         tanh(0, 1)
         apply_gain(0, 0)
-        cast_w(1, 1, ["scalar"])
-        cast_w(1, 2, ["vector", "vector"])
+        cast_w(1, 1, ["vector"])
+        cast_w(1, 2, ["scalar", "scalar"])
         quant_h(0, 0)
-        quant_w(1, 2)
         quant_w(1, 1)
+        for t in range(PACK):
+            quant_w_slot(1, KA - 1, t)
         for j in range(JH):
             for t in range(PACK):
                 for a in range(KA):
                     mm1(1, j, t, a)
-        gain_on_scalar(0, 1)
+        gain_on_scalar(0, 1, 1)
         tanh(1, 0)
         nc.vector.tensor_copy(out=v2_w[0][:], in_=tab2_w[0][:].indirect(offs2_t[:]))
         interleave(0, 1)
-        gain_on_scalar(1, 0)
         nc.vector.tensor_copy(out=v2_s[:], in_=tab2_s[:].indirect(offs2_t[:]))
         quant_h(0, 1)
         tanh(1, 1)
         nc.vector.tensor_copy(out=v2_w[1][:], in_=tab2_w[1][:].indirect(offs2_t[:]))
-        interleave(1, 0)
+        apply_gain(1, 0)
+        gain_on_scalar(1, 1, 1)
         quant_h(1, 0)
-        apply_gain(1, 1)
+        interleave(1, 1)
         for m in range(MT):
             for kind in range(2):
                 for b in range(HB):
                     mm2(m, 0, kind, b)
             take_d(m, 0)
         quant_h(1, 1)
+        nc.scalar.activation(out=ntemp_t[:], in_=temp_t[:], func=ACT.Copy, scale=-1.0)
         for m in range(MT):
             take_e(m, 0)
         for m in range(MT):
@@ -297,7 +324,7 @@ def tile_list_gravestone_kin_scores_kernel(
             take_d(m, 1)
             take_e(m, 1)
             row_max(m)
+            make_bias(m)
             exp_look(m)
-            if m > 0:
-                finish(m - 1)
-        finish(MT - 1)
+        for m in range(MT):
+            finish(m, (0, 384, NP) if m == MT - 1 else (0, NP))

@@ -80,7 +80,7 @@ def tile_list_gravestone_kin_scores_kernel(
         def load_w(b, a, pieces=1):
             width = KP // pieces
             for x in range(pieces):
-                tag, bufs = ("w_last0", 1) if (b, a, x) == (1, KA - 1, 1) else (f"w_raw{pieces}", 4)
+                tag, bufs = ("w_last0", 1) if (b, a, x) == (1, KA - 1, 1) else (f"w_raw{pieces}", 5 if pieces == 1 else 4)
                 w_raw[b, a, x] = ring.tile([P, PACK, width], F32, name="w_raw", tag=tag, bufs=bufs)
                 c0 = b * KP + x * width
                 nc.sync.dma_start(
@@ -214,18 +214,27 @@ def tile_list_gravestone_kin_scores_kernel(
             for c0, c1 in zip(cuts, cuts[1:]):
                 width = c1 - c0
                 cols = slice(c0, c1)
-                prod = ring.tile([P, width], F32, name="prod", tag="w_raw1", bufs=4)
+                prod = ring.tile([P, width], F32, name="prod", tag="w_raw1", bufs=5)
                 nc.vector.tensor_tensor(
                     out=prod[:], in0=d_t[m][:].indirect(pos2_t[:, c0 // 16 : c1 // 16]),
                     in1=look[m][:, cols], op=ALU.mult,
                 )
-                res = ring.tile([P, width], F32, name="res", bufs=5)
-                nc.scalar.activation(out=res[:], in_=prod[:], func=ACT.Identity, bias=kin_t[:, m : m + 1])
-                nc.sync.dma_start(out=out[m * P : (m + 1) * P, cols], in_=res[:])
+                nc.scalar.activation(out=prod[:], in_=prod[:], func=ACT.Identity, bias=kin_t[:, m : m + 1])
+                nc.sync.dma_start(out=out[m * P : (m + 1) * P, cols], in_=prod[:])
 
         nc.gpsimd.memset(tab_s[:].bitcast(I32), 0)
         nc.gpsimd.memset(tab2_s[:].bitcast(I32), 0)
+        for q in range(4):
+            nc.gpsimd.dma_start(
+                out=tab2_s[32 * q : 32 * q + 4 * HB, :].bitcast(I32),
+                in_=tab2_scales[:, 4 * q : 4 * q + 4, :].bitcast(I32),
+            )
         nc.gpsimd.memset(w4_s[:].bitcast(I32), 0)
+        for q in range(4):
+            nc.gpsimd.dma_start(
+                out=w4_s[32 * q : 32 * q + 4, :].bitcast(I32).rearrange("r (b c) -> r b c", b=HB),
+                in_=w4_scales[:, 4 * q : 4 * q + 4, :].bitcast(I32).rearrange("b r c -> r b c"),
+            )
         nc.sync.dma_start(out=tab_w[0][:].bitcast(I32), in_=words(tab_words[0]))
         nc.sync.dma_start(offs_t[:], offs)
         load_w(0, 0)
@@ -235,9 +244,10 @@ def tile_list_gravestone_kin_scores_kernel(
                 in_=tab_scales[:, 4 * q : 4 * q + 4, :].bitcast(I32),
             )
         nc.sync.dma_start(out=tab_w[1][:].bitcast(I32), in_=words(tab_words[1]))
+        nc.sync.dma_start(offs2_t[:], offs2)
         load_w(0, 1)
+        load_w(0, 2)
         nc.sync.dma_start(out=tab_w[2][:].bitcast(I32), in_=words(tab_words[2]))
-        load_w(0, 2, 2)
         nc.sync.dma_start(out=b1_t[:].rearrange("p (b i) -> p b i", i=PACK), in_=b1.rearrange("(b p i) -> p b i", p=P, i=PACK))
         load_w(1, 0)
         nc.sync.dma_start(out=gain_t[:].rearrange("p (b i) -> p b i", i=PACK), in_=gain.rearrange("(b p i) -> p b i", p=P, i=PACK))
@@ -249,32 +259,21 @@ def tile_list_gravestone_kin_scores_kernel(
         gather_words(1, 0, JH)
         cast_w(0, 1, ["scalar", "vector"])
         quant_w(0, 1)
+        cast_w(0, 2, ["scalar", "vector"])
+        quant_w(0, 2)
         gather_words(2, 0, 1)
-        cast_w(0, 2, ["scalar", "scalar"])
-        for t in range(PACK):
-            quant_w_slot(0, KA - 1, t)
         gather_words(2, 1, 2)
+        nc.vector.tensor_copy(out=v2_s[:], in_=tab2_s[:].indirect(offs2_t[:]))
         for j in range(JH):
             for a in range(KA):
                 for t in range(PACK):
                     mm1(0, j, t, a)
         load_w(1, 1)
         load_w(1, 2, 2)
-        nc.sync.dma_start(offs2_t[:], offs2)
         nc.sync.dma_start(out=tab2_w[0][:].bitcast(I32), in_=words(tab2_words[0]))
-        for q in range(4):
-            nc.sync.dma_start(
-                out=tab2_s[32 * q : 32 * q + 4 * HB, :].bitcast(I32),
-                in_=tab2_scales[:, 4 * q : 4 * q + 4, :].bitcast(I32),
-            )
         nc.sync.dma_start(out=tab2_w[1][:].bitcast(I32), in_=words(tab2_words[1]))
         for b in range(HB):
             nc.sync.dma_start(out=w4_w[b][:].bitcast(I32), in_=w4_words[b].bitcast(I32))
-        for q in range(4):
-            nc.sync.dma_start(
-                out=w4_s[32 * q : 32 * q + 4, :].bitcast(I32).rearrange("r (b c) -> r b c", b=HB),
-                in_=w4_scales[:, 4 * q : 4 * q + 4, :].bitcast(I32).rearrange("b r c -> r b c"),
-            )
         nc.sync.dma_start(pos1_t[:], pos1)
         nc.sync.dma_start(pos2_t[:], pos2)
         with nc.allow_non_contiguous_dma(reason="one value a partition"):
@@ -300,7 +299,6 @@ def tile_list_gravestone_kin_scores_kernel(
         tanh(1, 0)
         nc.vector.tensor_copy(out=v2_w[0][:], in_=tab2_w[0][:].indirect(offs2_t[:]))
         interleave(0, 1)
-        nc.vector.tensor_copy(out=v2_s[:], in_=tab2_s[:].indirect(offs2_t[:]))
         quant_h(0, 1)
         tanh(1, 1)
         nc.vector.tensor_copy(out=v2_w[1][:], in_=tab2_w[1][:].indirect(offs2_t[:]))

from contextlib import ExitStack

import concourse.mybir as mybir

K, T, S, H, T3, S2, NP = 1536, 2048, 1024, 1024, 2048, 512, 512
FLOPS = 2 * K * H * S + 2 * 2 * H * S2 * S

F32 = mybir.dt.float32
BF16 = mybir.dt.bfloat16
I32 = mybir.dt.int32
U32 = mybir.dt.uint32
U16 = mybir.dt.uint16
U8 = mybir.dt.uint8
FP8X4 = mybir.dt.float8_e4m3fn_x4
FP4X4 = mybir.dt.float4_e2m1fn_x4
ALU = mybir.AluOpType
ACT = mybir.ActivationFunctionType

P = 128
PACK = 4
KP = 512
N = 512
KA = K // KP
HB = H // KP
JH = S // N
MT = S2 // P


def tile_list_gravestone_kin_scores_kernel(
    tc, tab_words, tab_scales, offs, w1, b1, gain, tab2_words, tab2_scales, offs2,
    w4_words, w4_scales, pos1, pos2, temp, kin, out,
):
    nc = tc.nc
    with ExitStack() as ctx:
        keep = ctx.enter_context(tc.tile_pool(name="keep", bufs=1))
        ring = ctx.enter_context(tc.tile_pool(name="ring", bufs=2))
        psum = ctx.enter_context(tc.psum_pool(name="psum", bufs=1))

        def held(name, shape, dtype):
            return keep.tile(shape, dtype, name=name, align_bytes=64)

        def bank(k):
            return psum.tile([P, N], F32, name=f"bank{k}", tag=f"bank{k}")

        offs_t = held("offs_t", [P, S // 16], U16)
        offs2_t = held("offs2_t", [P, S2 // 16], U16)
        pos1_t = held("pos1_t", [P, NP // 16], U16)
        pos2_t = held("pos2_t", [P, NP // 16], U16)

        tab_w = [held(f"tab_w{a}", [P, T], U32) for a in range(KA)]
        tab_s = held("tab_s", [P, T], U8)
        tab2_w = [held(f"tab2_w{b}", [P, T3], U32) for b in range(HB)]
        tab2_s = held("tab2_s", [P, T3], U8)
        w4_w = [held(f"w4_w{b}", [P, 2 * S2], U8) for b in range(HB)]
        w4_s = held("w4_s", [P, HB * S2], U8)
        b1_t = held("b1_t", [P, HB * PACK], F32)
        gain_t = held("gain_t", [P, HB * PACK], F32)
        temp_t = held("temp_t", [P, MT], F32)
        kin_t = held("kin_t", [P, MT], F32)
        bias_t = held("bias_t", [P, MT], F32)
        ntemp_t = held("ntemp_t", [P, MT], F32)
        top_t = [held(f"top_t{m}", [P, 1], F32) for m in range(MT)]

        v_w = [held(f"v_w{a}", [P, S], U32) for a in range(KA)]
        v_s = held("v_s", [P, S], U8)
        v2_w = [held(f"v2_w{b}", [P, S2], U32) for b in range(HB)]
        v2_s = held("v2_s", [P, S2], U8)
        w_c = {(b, a): held(f"w_c{b}{a}", [P, KP], U32) for b in range(HB) for a in range(KA)}
        w_s = {(b, a): held(f"w_s{b}{a}", [P, KP], U8) for b in range(HB) for a in range(KA)}
        h_c = {(b, j): held(f"h_c{b}{j}", [P, N], U32) for b in range(HB) for j in range(JH)}
        h_s = {(b, j): held(f"h_s{b}{j}", [P, N], U8) for b in range(HB) for j in range(JH)}
        d_t = [held(f"d_t{m}", [P, S], F32) for m in range(MT)]
        e_t = [held(f"e_t{m}", [P, S], F32) for m in range(MT)]

        w_raw, w_bf, th, hp, hb, acc1, acc2, look = {}, {}, {}, {}, {}, {}, {}, {}

        def words(dram):
            return dram.rearrange("p t i -> p (t i)").bitcast(I32)

        def load_w(b, a, pieces=1):
            width = KP // pieces
            for x in range(pieces):
                tag, bufs = ("w_last0", 1) if (b, a, x) == (1, KA - 1, 1) else (f"w_raw{pieces}", 5 if pieces == 1 else 4)
                w_raw[b, a, x] = ring.tile([P, PACK, width], F32, name="w_raw", tag=tag, bufs=bufs)
                c0 = b * KP + x * width
                nc.sync.dma_start(
                    out=w_raw[b, a, x][:],
                    in_=w1[a * KP : (a + 1) * KP, c0 : c0 + width].rearrange("(p i) c -> p i c", i=PACK),
                )

        def cast_w(b, a, engines):
            tag, bufs = ("w_bf10", 1) if (b, a) == (1, 0) else ("w_bf", 3)
            w_bf[b, a] = ring.tile([P, PACK * KP], BF16, name="w_bf", tag=tag, bufs=bufs, align_bytes=64)
            rows = P // len(engines)
            for x, engine in enumerate(engines):
                if (b, a, 1) in w_raw:
                    src = w_raw[b, a, x][:].rearrange("p i (m t) -> p m i t", t=PACK)
                else:
                    src = w_raw[b, a, 0][:].rearrange("p i (m t) -> p m i t", t=PACK)[:, x * rows : (x + 1) * rows]
                dst = w_bf[b, a][:].rearrange("p (t m i) -> p m i t", t=PACK, i=PACK)[:, x * rows : (x + 1) * rows]
                if engine == "scalar":
                    nc.scalar.copy(out=dst, in_=src)
                else:
                    nc.vector.tensor_copy(out=dst, in_=src)

        def quant_w(b, a):
            nc.vector.quantize_mx(out=w_c[b, a][:].bitcast(FP8X4), scales=w_s[b, a][:], in_=w_bf[b, a][:])

        def quant_w_slot(b, a, t):
            nc.vector.quantize_mx(
                out=w_c[b, a][:, t * P : (t + 1) * P].bitcast(FP8X4),
                scales=w_s[b, a][:, t * P : (t + 1) * P],
                in_=w_bf[b, a][:, t * KP : (t + 1) * KP],
            )

        def gather_words(a, j0, j1):
            nc.vector.tensor_copy(
                out=v_w[a][:, j0 * N : j1 * N], in_=tab_w[a][:].indirect(offs_t[:, j0 * N // 16 : j1 * N // 16])
            )

        def mm1(b, j, t, a):
            if a == 0:
                acc1[b, j, t] = bank(PACK * j + t)
            cols = slice(t * P, (t + 1) * P)
            nc.tensor.matmul_mx(
                out=acc1[b, j, t][:],
                lhsT=w_c[b, a][:, cols].bitcast(FP8X4),
                lhsT_scale=w_s[b, a][:, cols],
                rhs=v_w[a][:, j * N : (j + 1) * N].bitcast(FP8X4),
                rhs_scale=v_s[4 * a : P, j * N : (j + 1) * N],
                start=(a == 0),
                stop=(a == KA - 1),
            )

        def tanh(b, j):
            th[b, j] = ring.tile([P, PACK, N], F32, name="th", bufs=3)
            for t in range(PACK):
                c = b * PACK + t
                nc.scalar.activation(out=th[b, j][:, t, :], in_=acc1[b, j, t][:], func=ACT.Tanh, bias=b1_t[:, c : c + 1])

        def apply_gain(b, j):
            tag, bufs = ("w_bf10", 1) if (b, j) == (0, 0) else ("hb", 2)
            hb[b, j] = ring.tile([P, PACK * N], BF16, name="hb", tag=tag, bufs=bufs, align_bytes=64)
            g = gain_t[:, b * PACK : (b + 1) * PACK].rearrange("p (c t u) -> p c t u", c=1, u=1)
            nc.vector.tensor_tensor(
                out=hb[b, j][:].rearrange("p (c u t) -> p c t u", t=PACK, u=4),
                in0=th[b, j][:].rearrange("p t (c u) -> p c t u", u=4),
                in1=g.to_broadcast([P, N // 4, PACK, 4]),
                op=ALU.mult,
            )

        def gain_on_scalar(b, j, on_vector):
            hp[b, j] = ring.tile([P, PACK, N], BF16, name="hp", tag=f"w_last{b}", bufs=1)
            for t in range(PACK):
                c = b * PACK + t
                if t < PACK - on_vector:
                    nc.scalar.activation(out=hp[b, j][:, t, :], in_=th[b, j][:, t, :], func=ACT.Copy, scale=gain_t[:, c : c + 1])
                else:
                    nc.vector.tensor_scalar(
                        out=hp[b, j][:, t, :], in0=th[b, j][:, t, :], scalar1=gain_t[:, c : c + 1], scalar2=None, op0=ALU.mult
                    )

        def interleave(b, j):
            hb[b, j] = ring.tile([P, PACK * N], BF16, name="hb", tag="hb", bufs=2, align_bytes=64)
            nc.vector.tensor_copy(
                out=hb[b, j][:].rearrange("p (c u t) -> p c t u", t=PACK, u=4),
                in_=hp[b, j][:].rearrange("p t (c u) -> p c t u", u=4),
            )

        def quant_h(b, j):
            nc.vector.quantize_mx(out=h_c[b, j][:].bitcast(FP8X4), scales=h_s[b, j][:], in_=hb[b, j][:])

        def mm2(m, j, kind, b):
            if b == 0:
                acc2[m, j, kind] = bank(2 * m + kind)
            cols = slice(m * P, (m + 1) * P)
            if kind == 0:
                lhsT = w4_w[b][:, 2 * m * P : 2 * (m + 1) * P].bitcast(FP4X4)
                lhsT_scale = w4_s[:, b * S2 + m * P : b * S2 + (m + 1) * P]
            else:
                lhsT = v2_w[b][:, cols].bitcast(FP8X4)
                lhsT_scale = v2_s[4 * b : P, cols]
            nc.tensor.matmul_mx(
                out=acc2[m, j, kind][:],
                lhsT=lhsT,
                lhsT_scale=lhsT_scale,
                rhs=h_c[b, j][:].bitcast(FP8X4),
                rhs_scale=h_s[b, j][:],
                start=(b == 0),
                stop=(b == HB - 1),
            )

        def take_d(m, j):
            nc.scalar.copy(out=d_t[m][:, j * N : (j + 1) * N], in_=acc2[m, j, 0][:])

        def take_e(m, j):
            cols = slice(j * N, (j + 1) * N)
            nc.vector.tensor_tensor(out=e_t[m][:, cols], in0=acc2[m, j, 1][:], in1=d_t[m][:, cols], op=ALU.max)

        def row_max(m):
            nc.vector.reduce_max(out=top_t[m][:], in_=e_t[m][:], axis=mybir.AxisListType.X)

        def make_bias(m):
            nc.scalar.activation(out=bias_t[:, m : m + 1], in_=top_t[m][:], func=ACT.Copy, scale=ntemp_t[:, m : m + 1])

        def exp_look(m):
            look[m] = ring.tile([P, NP], F32, name="look", tag="w_raw2", bufs=4)
            nc.scalar.activation(
                out=look[m][:], in_=e_t[m][:].indirect(pos1_t[:]), func=ACT.Exp,
                bias=bias_t[:, m : m + 1], scale=temp_t[:, m : m + 1],
            )

        def finish(m, cuts=(0, NP)):
            for c0, c1 in zip(cuts, cuts[1:]):
                width = c1 - c0
                cols = slice(c0, c1)
                prod = ring.tile([P, width], F32, name="prod", tag="w_raw1", bufs=5)
                nc.vector.tensor_tensor(
                    out=prod[:], in0=d_t[m][:].indirect(pos2_t[:, c0 // 16 : c1 // 16]),
                    in1=look[m][:, cols], op=ALU.mult,
                )
                nc.scalar.activation(out=prod[:], in_=prod[:], func=ACT.Identity, bias=kin_t[:, m : m + 1])
                nc.sync.dma_start(out=out[m * P : (m + 1) * P, cols], in_=prod[:])

        nc.gpsimd.memset(tab_s[:].bitcast(I32), 0)
        nc.gpsimd.memset(tab2_s[:].bitcast(I32), 0)
        for q in range(4):
            nc.gpsimd.dma_start(
                out=tab2_s[32 * q : 32 * q + 4 * HB, :].bitcast(I32),
                in_=tab2_scales[:, 4 * q : 4 * q + 4, :].bitcast(I32),
            )
        nc.gpsimd.memset(w4_s[:].bitcast(I32), 0)
        for q in range(4):
            nc.gpsimd.dma_start(
                out=w4_s[32 * q : 32 * q + 4, :].bitcast(I32).rearrange("r (b c) -> r b c", b=HB),
                in_=w4_scales[:, 4 * q : 4 * q + 4, :].bitcast(I32).rearrange("b r c -> r b c"),
            )
        nc.sync.dma_start(out=tab_w[0][:].bitcast(I32), in_=words(tab_words[0]))
        nc.sync.dma_start(offs_t[:], offs)
        load_w(0, 0)
        for q in range(4):
            nc.sync.dma_start(
                out=tab_s[32 * q : 32 * q + 4 * KA, :].bitcast(I32),
                in_=tab_scales[:, 4 * q : 4 * q + 4, :].bitcast(I32),
            )
        nc.sync.dma_start(out=tab_w[1][:].bitcast(I32), in_=words(tab_words[1]))
        nc.sync.dma_start(offs2_t[:], offs2)
        load_w(0, 1)
        load_w(0, 2)
        nc.sync.dma_start(out=tab_w[2][:].bitcast(I32), in_=words(tab_words[2]))
        nc.sync.dma_start(out=b1_t[:].rearrange("p (b i) -> p b i", i=PACK), in_=b1.rearrange("(b p i) -> p b i", p=P, i=PACK))
        load_w(1, 0)
        nc.sync.dma_start(out=gain_t[:].rearrange("p (b i) -> p b i", i=PACK), in_=gain.rearrange("(b p i) -> p b i", p=P, i=PACK))

        gather_words(0, 0, JH)
        nc.vector.tensor_copy(out=v_s[:], in_=tab_s[:].indirect(offs_t[:]))
        cast_w(0, 0, ["scalar"])
        quant_w(0, 0)
        gather_words(1, 0, JH)
        cast_w(0, 1, ["scalar", "vector"])
        quant_w(0, 1)
        cast_w(0, 2, ["scalar", "vector"])
        quant_w(0, 2)
        gather_words(2, 0, 1)
        gather_words(2, 1, 2)
        nc.vector.tensor_copy(out=v2_s[:], in_=tab2_s[:].indirect(offs2_t[:]))
        for j in range(JH):
            for a in range(KA):
                for t in range(PACK):
                    mm1(0, j, t, a)
        load_w(1, 1)
        load_w(1, 2, 2)
        nc.sync.dma_start(out=tab2_w[0][:].bitcast(I32), in_=words(tab2_words[0]))
        nc.sync.dma_start(out=tab2_w[1][:].bitcast(I32), in_=words(tab2_words[1]))
        for b in range(HB):
            nc.sync.dma_start(out=w4_w[b][:].bitcast(I32), in_=w4_words[b].bitcast(I32))
        nc.sync.dma_start(pos1_t[:], pos1)
        nc.sync.dma_start(pos2_t[:], pos2)
        with nc.allow_non_contiguous_dma(reason="one value a partition"):
            nc.sync.dma_start(out=temp_t[:], in_=temp.rearrange("(m p) -> p m", p=P))
            nc.sync.dma_start(out=kin_t[:], in_=kin.rearrange("(m p) -> p m", p=P))

        tanh(0, 0)
        cast_w(1, 0, ["vector"])
        quant_w(1, 0)
        tanh(0, 1)
        apply_gain(0, 0)
        cast_w(1, 1, ["vector"])
        cast_w(1, 2, ["scalar", "scalar"])
        quant_h(0, 0)
        quant_w(1, 1)
        for t in range(PACK):
            quant_w_slot(1, KA - 1, t)
        for j in range(JH):
            for t in range(PACK):
                for a in range(KA):
                    mm1(1, j, t, a)
        gain_on_scalar(0, 1, 1)
        tanh(1, 0)
        nc.vector.tensor_copy(out=v2_w[0][:], in_=tab2_w[0][:].indirect(offs2_t[:]))
        interleave(0, 1)
        quant_h(0, 1)
        tanh(1, 1)
        nc.vector.tensor_copy(out=v2_w[1][:], in_=tab2_w[1][:].indirect(offs2_t[:]))
        apply_gain(1, 0)
        gain_on_scalar(1, 1, 1)
        quant_h(1, 0)
        interleave(1, 1)
        for m in range(MT):
            for kind in range(2):
                for b in range(HB):
                    mm2(m, 0, kind, b)
            take_d(m, 0)
        quant_h(1, 1)
        nc.scalar.activation(out=ntemp_t[:], in_=temp_t[:], func=ACT.Copy, scale=-1.0)
        for m in range(MT):
            take_e(m, 0)
        for m in range(MT):
            for kind in range(2):
                for b in range(HB):
                    mm2(m, 1, kind, b)
            take_d(m, 1)
            take_e(m, 1)
            row_max(m)
            make_bias(m)
            exp_look(m)
        for m in range(MT):
            finish(m, (0, 384, NP) if m == MT - 1 else (0, NP))
